import numpy as np
import ml_dtypes


def mxq(x, axis, fmt="e4m3"):
    dtype, down = {"e4m3": (ml_dtypes.float8_e4m3fn, 7), "e5m2": (ml_dtypes.float8_e5m2, 14)}[fmt]
    v = np.moveaxis(np.asarray(x, np.float32).astype(ml_dtypes.bfloat16).astype(np.float64), axis, -1)
    blocks = v.reshape(v.shape[:-1] + (-1, 32))
    amax = np.abs(blocks).max(-1, keepdims=True)
    byte = np.maximum(np.where(amax > 0, np.frexp(amax)[1] - 1 + 127, 0) - down, 1)
    scale = np.exp2(byte - 127.0)
    codes = (blocks / scale).astype(np.float32).astype(dtype).astype(np.float64)
    return np.moveaxis((codes * scale).reshape(v.shape), -1, axis)


WIDE = False


def mx_kscale(k):
    if not WIDE:
        return np.ones(k)
    levels = np.array([10, -10, 5, -5, 0])
    if k % 512:
        return np.exp2(np.random.permutation(np.resize(levels, k // 32))).repeat(32)
    a = np.empty((k // 512, 16))
    for p in range(k // 512):
        a[p, :8] = np.random.permutation(np.resize(levels, 8))
        for g in range(8):
            far = levels[np.abs(levels - a[p, g]) >= 10]
            a[p, g + 8] = far[np.random.randint(len(far))]
    return np.exp2(a.ravel()).repeat(32)


def f64(x):
    return np.asarray(x).astype(np.float64)


def striped(idx):
    return np.tile(idx.reshape(-1, 16).T, (8, 1)).astype(np.uint16)


def unstriped(offs):
    return offs[:16].T.reshape(-1).astype(np.int64)


def pack_weight(w):
    k, n = w.shape
    w = f64(np.asarray(w, np.float32).astype(ml_dtypes.bfloat16)).reshape(k // 32, 32, n)
    amax = np.abs(w).max(1)
    byte = np.clip(np.where(amax > 0, np.frexp(amax)[1] - 1 + 127 - 7, 1), 1, 254)
    scaled = (w * np.exp2(127.0 - byte)[:, None, :]).reshape(k, n).astype(np.float32)
    words = np.ascontiguousarray(scaled.reshape(k // 512, 128, 4, n).transpose(0, 1, 3, 2)).astype(ml_dtypes.float8_e4m3fn).view(np.uint8)
    return words, np.ascontiguousarray(byte.astype(np.uint8).reshape(k // 512, 16, n))


def unpack_weight(words, scales):
    g, p, n, _ = words.shape
    vals = np.ascontiguousarray(words).view(ml_dtypes.float8_e4m3fn).astype(np.float64) * np.repeat(np.exp2(scales.astype(np.float64) - 127.0), 8, axis=1)[..., None]
    return vals.transpose(0, 1, 3, 2).reshape(g * 512, n)


K, T, S, D, N, U = 1024, 1024, 512, 4, 256, 1024
P = 2 ** 7


def setup_inputs():
    n = np.random.standard_normal
    s = mx_kscale(K)[:, None]
    packed_xT = pack_weight(n((K, T)) * s)
    return {
        "x_words": packed_xT[0],
        "x_scales": packed_xT[1],
        "w1": (n((K, N)) / np.sqrt(K) / s).astype(np.float32),
        "lr": (np.tile(0.3 * n(U), (P, 1))).astype(np.float32),
        "lo": (np.tile(np.random.uniform(0.75, 0.85, U), (P, 1))).astype(np.float32),
        "hi": (np.tile(np.random.uniform(1.15, 1.3, U), (P, 1))).astype(np.float32),
        "offs": striped(np.random.permutation(T)[:S]),
        "ans": striped(np.random.permutation(np.concatenate([np.arange(S), np.random.randint(0, S, U - S)]))),
    }


def reference(x_words, x_scales, w1, lr, lo, hi, offs, ans):
    xq = unpack_weight(x_words, x_scales)[:, unstriped(offs)]
    y = mxq(f64(w1), 0, "e4m3").T @ xq
    my = y.reshape(len(y), -1, D).mean(axis=2)
    dd = y - np.repeat(my, D, axis=1)
    d2 = (dd) ** 2
    sd = np.sqrt(d2.reshape(len(d2), -1, D).mean(axis=2) + 0.1)
    adv = dd / np.repeat(sd, D, axis=1)
    at = adv[:, unstriped(ans)]
    ratio = np.exp(f64(lr)[:1])
    clip = np.minimum(np.maximum(ratio, f64(lo)[:1]), f64(hi)[:1])
    return np.minimum(at * ratio, at * clip)

@@ -1,0 +1,223 @@
+from contextlib import ExitStack
+
+import concourse.mybir as mybir
+from concourse.masks import make_identity
+
+F32 = mybir.dt.float32
+BF16 = mybir.dt.bfloat16
+I32 = mybir.dt.int32
+U32 = mybir.dt.uint32
+U16 = mybir.dt.uint16
+U8 = mybir.dt.uint8
+FP8X4 = mybir.dt.float8_e4m3fn_x4
+ALU = mybir.AluOpType
+ACT = mybir.ActivationFunctionType
+AX = mybir.AxisListType
+
+P = 128
+K, T, S, D, N, U = 1024, 1024, 512, 4, 256, 1024
+PASSES = 2
+HALF = S // 2
+FLOPS = 2 * K * N * S
+BYTES = 2 * P * T * 4 + 2 * 16 * T + K * N * 4 + 3 * U * 4 + P * (S + U) // 8 + N * U * 4
+
+
+def tile_picked_ygrpo_clip_p_kernel(tc, x_words, x_scales, w1, lr, lo, hi, offs, ans, out):
+    nc = tc.nc
+    with ExitStack() as ctx:
+        keep = ctx.enter_context(tc.tile_pool(name="keep", bufs=1))
+        psum = ctx.enter_context(tc.psum_pool(name="psum", bufs=1))
+
+        offs_t = keep.tile([P, S // 16], U16, name="offs_t")
+        ans_t = keep.tile([P, U // 16], U16, name="ans_t")
+        xs = keep.tile([P, T], U8, name="xs", align_bytes=64)
+        xw = [keep.tile([P, T], U32, name=f"xw{o}", align_bytes=64) for o in range(PASSES)]
+        wraw = [keep.tile([P, 4, N], F32, name=f"wraw{o}", align_bytes=64) for o in range(PASSES)]
+        lr_rows = keep.tile([8, P], F32, name="lr_rows", align_bytes=64)
+        ratio_rows = keep.tile([8, P], F32, name="ratio_rows", align_bytes=64)
+        ident = keep.tile([P, P], F32, name="ident", align_bytes=64)
+        adv = [keep.tile([P, S], F32, name=f"adv{b}", align_bytes=64) for b in range(2)]
+
+        nc.gpsimd.memset(xs[:].bitcast(I32), 0)
+        make_identity(nc, ident[:])
+
+        def load_x(queue, o):
+            queue.dma_start(out=xw[o][:].bitcast(I32), in_=x_words[o].rearrange("p c r -> p (c r)").bitcast(I32))
+
+        def load_w(queue, o):
+            queue.dma_start(out=wraw[o][:], in_=w1[512 * o : 512 * (o + 1), :].rearrange("(p j) c -> p j c", j=4))
+
+        nc.sync.dma_start(offs_t[:], offs)
+        nc.sync.dma_start(out=lr_rows[:], in_=lr[0].rearrange("(b n) -> b n", n=P))
+        load_x(nc.sync, 0)
+        for q in range(4):
+            nc.sync.dma_start(out=xs[32 * q : 32 * q + 8, :].bitcast(I32), in_=x_scales[:, 4 * q : 4 * q + 4, :].bitcast(I32))
+        load_w(nc.sync, 0)
+        load_w(nc.sync, 1)
+        load_x(nc.sync, 1)
+        nc.sync.dma_start(ans_t[:], ans)
+        nc.scalar.activation(ratio_rows[:], lr_rows[:], ACT.Exp)
+        warm = keep.tile([8, 1], F32, name="warm")
+        nc.scalar.activation(warm[:], ratio_rows[:, 0:1], ACT.Abs_reciprocal_sqrt)
+
+        wbf = [keep.tile([P, 4 * N], BF16, name=f"wbf{o}", align_bytes=64) for o in range(PASSES)]
+        wq = [keep.tile([P, N], U32, name=f"wq{o}", align_bytes=64) for o in range(PASSES)]
+        ws = [keep.tile([P, N], U8, name=f"ws{o}", align_bytes=64) for o in range(PASSES)]
+
+        def weave(copy, o, c0, c1):
+            copy(
+                wbf[o][:, 4 * c0 : 4 * c1].rearrange("p (c i t) -> p c t i", i=4, t=4),
+                wraw[o][:, :, c0:c1].rearrange("p t (c i) -> p c t i", i=4),
+            )
+
+        def quant(o, c0, c1):
+            nc.vector.quantize_mx(out=wq[o][:, c0:c1].bitcast(FP8X4), scales=ws[o][:, c0:c1], in_=wbf[o][:, 4 * c0 : 4 * c1])
+
+        gs = keep.tile([P, S], U8, name="gs", align_bytes=64)
+        gw0 = keep.tile([P, S], U32, name="gw0", align_bytes=64)
+        gw1 = [keep.tile([P, HALF], U32, name=f"gw1{h}", align_bytes=64) for h in range(2)]
+
+        nc.vector.tensor_copy(gs[:], xs[:].indirect(offs_t[:]))
+        nc.vector.tensor_copy(gw0[:], xw[0][:].indirect(offs_t[:]))
+        weave(nc.scalar.copy, 0, 0, N)
+        quant(0, 0, N)
+        weave(nc.scalar.copy, 1, 0, P)
+        weave(nc.vector.tensor_copy, 1, P, N)
+        quant(1, 0, P)
+        quant(1, P, N)
+        for h in range(2):
+            nc.vector.tensor_copy(gw1[h][:], xw[1][:].indirect(offs_t[:, h * HALF // 16 : (h + 1) * HALF // 16]))
+
+        def product(acc, b, h):
+            half = slice(h * HALF, (h + 1) * HALF)
+            for o, words in enumerate((gw0[:, half], gw1[h][:])):
+                nc.tensor.matmul_mx(
+                    out=acc,
+                    lhsT=wq[o][:, b * P : (b + 1) * P].bitcast(FP8X4),
+                    lhsT_scale=ws[o][:, b * P : (b + 1) * P],
+                    rhs=words.bitcast(FP8X4),
+                    rhs_scale=gs[4 * o : P, half],
+                    start=(o == 0),
+                    stop=(o == PASSES - 1),
+                )
+
+        G = S // D
+        y = [[psum.tile([P, HALF], F32, name=f"y{b}{h}", tag="work", bufs=6) for h in range(2)] for b in range(2)]
+        for h in range(2):
+            for b in range(2):
+                product(y[b][h][:], b, h)
+
+        tok = wraw[0][:, 0, 0:P]
+        nc.scalar.copy(tok[0:8, :], ratio_rows[:])
+        for i, src in ((1, lo), (2, hi)):
+            nc.sync.dma_start(out=tok[8 * i : 8 * i + 8, :], in_=src[0].rearrange("(b n) -> b n", n=P))
+        tok_ps = psum.tile([P, P], F32, name="tok_ps", tag="work", bufs=6)
+        nc.tensor.transpose(tok_ps[:], tok, ident[:])
+        tok_sb = keep.tile([P, 24], F32, name="tok_sb")
+        nc.scalar.copy(tok_sb[:], tok_ps[:, 0:24])
+
+        sums = [[keep.tile([P, G // 2], F32, name=f"sums{b}{h}") for h in range(2)] for b in range(2)]
+        dd = [keep.tile([P, G, D], F32, name=f"dd{b}") for b in range(2)]
+        d2 = [keep.tile([P, G, D], F32, name=f"d2{b}") for b in range(2)]
+        var = [keep.tile([P, G], F32, name=f"var{b}") for b in range(2)]
+        rs = [keep.tile([P, G], F32, name=f"rs{b}") for b in range(2)]
+        for h in range(2):
+            for b in range(2):
+                nc.vector.tensor_reduce(sums[b][h][:], y[b][h][:].rearrange("p (v d) -> p v d", d=D), AX.X, ALU.add)
+        for b in range(2):
+            for h in range(2):
+                groups = slice(h * G // 2, (h + 1) * G // 2)
+                nc.vector.scalar_tensor_tensor(
+                    dd[b][:, groups, :], sums[b][h][:].unsqueeze(2).to_broadcast([P, G // 2, D]), -1.0 / D,
+                    y[b][h][:].rearrange("p (v d) -> p v d", d=D), ALU.mult, ALU.add,
+                )
+                nc.scalar.activation(d2[b][:, groups, :], dd[b][:, groups, :], ACT.Square, scale=0.5)
+        for b in range(2):
+            nc.vector.tensor_reduce(var[b][:], d2[b][:], AX.X, ALU.add)
+            nc.scalar.activation(rs[b][:], var[b][:], ACT.Abs_reciprocal_sqrt, bias=0.1)
+
+        def normalise(b):
+            nc.vector.tensor_tensor(
+                adv[b][:].rearrange("p (v d) -> p v d", d=D), dd[b][:], rs[b][:].unsqueeze(2).to_broadcast([P, G, D]), ALU.mult
+            )
+
+        normalise(0)
+        ratio = tok_sb[:, 0:8]
+        above = keep.tile([P, 8], F32, name="above")
+        clip = keep.tile([P, 8], F32, name="clip")
+        kappa = keep.tile([P, 8], F32, name="kappa")
+        neg_clip = keep.tile([P, 8], F32, name="neg_clip")
+        nc.vector.tensor_tensor(above[:], ratio, tok_sb[:, 8:16], ALU.max)
+        nc.vector.tensor_tensor(clip[:], above[:], tok_sb[:, 16:24], ALU.min)
+        nc.vector.tensor_tensor(kappa[:], clip[:], ratio, ALU.subtract)
+        nc.scalar.mul(neg_clip[:], clip[:], -1.0)
+
+        def spread(col, bank):
+            for i in range(4):
+                nc.tensor.transpose(bank[:, i * P : (i + 1) * P], col[:, i : i + 1].to_broadcast([P, P]), ident[:])
+
+        ratio_ps = psum.tile([P, 4 * P], F32, name="ratio_ps")
+        spread(tok_sb[:, 4:8], ratio_ps)
+        clip_ps = psum.tile([P, 4 * P], F32, name="clip_ps")
+        spread(clip[:, 4:8], clip_ps)
+
+        def fetch(b, c0, c1):
+            g = keep.tile([P, c1 - c0], F32, name=f"g{b}_{c0}", align_bytes=64)
+            nc.vector.tensor_copy(g[:], adv[b][:].indirect(ans_t[:, c0 // 16 : c1 // 16]))
+            return g
+
+        def turn(b, c0, c1):
+            g = fetch(b, c0, c1)
+            width = c1 - c0
+            gt = psum.tile([P, width], F32, name=f"gt{b}_{c0}", tag="work", bufs=6)
+            for i in range(width // P):
+                nc.tensor.transpose(gt[:, i * P : (i + 1) * P], g[:, i * P : (i + 1) * P], ident[:])
+            over = keep.tile([P, width], F32, name=f"over{b}_{c0}", align_bytes=64)
+            lin = keep.tile([P, width], F32, name=f"lin{b}_{c0}", align_bytes=64)
+            for i in range(width // P):
+                t = c0 // P + i
+                cols = slice(i * P, (i + 1) * P)
+                nc.scalar.activation(over[:, cols], gt[:, cols], ACT.Relu, scale=kappa[:, t : t + 1])
+                nc.scalar.activation(lin[:, cols], gt[:, cols], ACT.Copy, scale=neg_clip[:, t : t + 1])
+            return b, c0, c1, over, lin
+
+        def turn_back(b, c0, c1, over, lin):
+            width = c1 - c0
+            back = psum.tile([P, width], F32, name=f"back{b}_{c0}", tag="work", bufs=6)
+            for i in range(width // P):
+                cols = slice(i * P, (i + 1) * P)
+                nc.tensor.matmul(back[:, cols], over[:, cols], ident[:], start=True, stop=False, is_transpose=True)
+                nc.tensor.matmul(back[:, cols], lin[:, cols], ident[:], start=False, stop=True, is_transpose=True)
+            return b, c0, c1, back
+
+        def leave(b, c0, c1, back):
+            o = keep.tile([P, c1 - c0], F32, name=f"o{b}_{c0}", align_bytes=64)
+            nc.scalar.mul(o[:], back[:], -1.0)
+            nc.sync.dma_start(out=out[P * b : P * (b + 1), c0:c1], in_=o[:])
+
+        def direct(b, chunks):
+            gs_, us, vs = [fetch(b, c0, c1) for c0, c1 in chunks], [], []
+            for (c0, c1), g in zip(chunks, gs_):
+                u = keep.tile([P, c1 - c0], F32, name=f"u{b}_{c0}", align_bytes=64)
+                nc.vector.tensor_tensor(u[:], g[:], ratio_ps[:, c0 - 512 : c1 - 512], ALU.mult)
+                v = keep.tile([P, c1 - c0], F32, name=f"v{b}_{c0}", align_bytes=64)
+                nc.vector.tensor_tensor(v[:], g[:], clip_ps[:, c0 - 512 : c1 - 512], ALU.mult)
+                us.append(u)
+                vs.append(v)
+            for (c0, c1), u, v in zip(chunks, us, vs):
+                o = keep.tile([P, c1 - c0], F32, name=f"o{b}_{c0}", align_bytes=64)
+                nc.vector.tensor_tensor(o[:], u[:], v[:], ALU.min)
+                nc.sync.dma_start(out=out[P * b : P * (b + 1), c0:c1], in_=o[:])
+
+        chunks = [(0, 0, 128), (0, 128, 384), (0, 384, 640), (0, 640, 896), (0, 896, 1024), (1, 0, 256), (1, 256, 384), (1, 384, 512)]
+        turned, backs = [], []
+        for k in range(len(chunks) + 2):
+            if k < len(chunks):
+                if chunks[k][:2] == (1, 0):
+                    normalise(1)
+                turned.append(turn(*chunks[k]))
+            if 1 <= k <= len(chunks):
+                backs.append(turn_back(*turned[k - 1]))
+            if k >= 2:
+                leave(*backs[k - 2])
+        direct(1, [(512, 768), (768, 1024)])

@@ -36,10 +36,11 @@ def tile_picked_ygrpo_clip_p_kernel(tc, x_words, x_scales, w1, lr, lo, hi, offs,
         lr_rows = keep.tile([8, P], F32, name="lr_rows", align_bytes=64)
         ratio_rows = keep.tile([8, P], F32, name="ratio_rows", align_bytes=64)
         ident = keep.tile([P, P], F32, name="ident", align_bytes=64)
-        adv = [keep.tile([P, S], F32, name=f"adv{b}", align_bytes=64) for b in range(2)]
+        adv = [keep.tile([P, S + 16 * b], F32, name=f"adv{b}", align_bytes=64) for b in range(2)]
 
         nc.gpsimd.memset(xs[:].bitcast(I32), 0)
         make_identity(nc, ident[:])
+        nc.gpsimd.memset(adv[1][:, S:], 0.0)
 
         def load_x(queue, o):
             queue.dma_start(out=xw[o][:].bitcast(I32), in_=x_words[o].rearrange("p c r -> p (c r)").bitcast(I32))
@@ -102,7 +103,7 @@ def tile_picked_ygrpo_clip_p_kernel(tc, x_words, x_scales, w1, lr, lo, hi, offs,
                 )
 
         G = S // D
-        y = [[psum.tile([P, HALF], F32, name=f"y{b}{h}", tag="work", bufs=6) for h in range(2)] for b in range(2)]
+        y = [[psum.tile([P, HALF], F32, name=f"y{b}{h}", tag=f"bank{2 * b + h}") for h in range(2)] for b in range(2)]
         for h in range(2):
             for b in range(2):
                 product(y[b][h][:], b, h)
@@ -111,7 +112,7 @@ def tile_picked_ygrpo_clip_p_kernel(tc, x_words, x_scales, w1, lr, lo, hi, offs,
         nc.scalar.copy(tok[0:8, :], ratio_rows[:])
         for i, src in ((1, lo), (2, hi)):
             nc.sync.dma_start(out=tok[8 * i : 8 * i + 8, :], in_=src[0].rearrange("(b n) -> b n", n=P))
-        tok_ps = psum.tile([P, P], F32, name="tok_ps", tag="work", bufs=6)
+        tok_ps = psum.tile([P, P], F32, name="tok_ps", tag="bank4")
         nc.tensor.transpose(tok_ps[:], tok, ident[:])
         tok_sb = keep.tile([P, 24], F32, name="tok_sb")
         nc.scalar.copy(tok_sb[:], tok_ps[:, 0:24])
@@ -124,6 +125,23 @@ def tile_picked_ygrpo_clip_p_kernel(tc, x_words, x_scales, w1, lr, lo, hi, offs,
         for h in range(2):
             for b in range(2):
                 nc.vector.tensor_reduce(sums[b][h][:], y[b][h][:].rearrange("p (v d) -> p v d", d=D), AX.X, ALU.add)
+        ratio = tok_sb[:, 0:8]
+        above = keep.tile([P, 8], F32, name="above")
+        clip = keep.tile([P, 8], F32, name="clip")
+        kappa = keep.tile([P, 8], F32, name="kappa")
+        neg_clip = keep.tile([P, 8], F32, name="neg_clip")
+        tiny = keep.tile([P, 8], F32, name="tiny")
+        base = keep.tile([P, 8], F32, name="base")
+        inv = keep.tile([P, 8], F32, name="inv")
+        rho = keep.tile([P, 8], F32, name="rho")
+        nc.vector.tensor_tensor(above[:], ratio, tok_sb[:, 8:16], ALU.max)
+        nc.vector.tensor_tensor(clip[:], above[:], tok_sb[:, 16:24], ALU.min)
+        nc.vector.tensor_scalar(tiny[:], clip[:], 0.0, 2.0**-64, ALU.is_equal, ALU.mult)
+        nc.vector.tensor_tensor(kappa[:], clip[:], ratio, ALU.subtract)
+        nc.vector.tensor_tensor(base[:], clip[:], tiny[:], ALU.add)
+        nc.scalar.mul(neg_clip[:], clip[:], -1.0)
+        nc.vector.reciprocal(inv[:], base[:])
+        nc.vector.tensor_tensor(rho[:], ratio, inv[:], ALU.mult)
         for b in range(2):
             for h in range(2):
                 groups = slice(h * G // 2, (h + 1) * G // 2)
@@ -138,28 +156,25 @@ def tile_picked_ygrpo_clip_p_kernel(tc, x_words, x_scales, w1, lr, lo, hi, offs,
 
         def normalise(b):
             nc.vector.tensor_tensor(
-                adv[b][:].rearrange("p (v d) -> p v d", d=D), dd[b][:], rs[b][:].unsqueeze(2).to_broadcast([P, G, D]), ALU.mult
+                adv[b][:, 0:S].rearrange("p (v d) -> p v d", d=D), dd[b][:], rs[b][:].unsqueeze(2).to_broadcast([P, G, D]), ALU.mult
             )
 
         normalise(0)
-        ratio = tok_sb[:, 0:8]
-        above = keep.tile([P, 8], F32, name="above")
-        clip = keep.tile([P, 8], F32, name="clip")
-        kappa = keep.tile([P, 8], F32, name="kappa")
-        neg_clip = keep.tile([P, 8], F32, name="neg_clip")
-        nc.vector.tensor_tensor(above[:], ratio, tok_sb[:, 8:16], ALU.max)
-        nc.vector.tensor_tensor(clip[:], above[:], tok_sb[:, 16:24], ALU.min)
-        nc.vector.tensor_tensor(kappa[:], clip[:], ratio, ALU.subtract)
-        nc.scalar.mul(neg_clip[:], clip[:], -1.0)
-
         def spread(col, bank):
             for i in range(4):
                 nc.tensor.transpose(bank[:, i * P : (i + 1) * P], col[:, i : i + 1].to_broadcast([P, P]), ident[:])
 
-        ratio_ps = psum.tile([P, 4 * P], F32, name="ratio_ps")
-        spread(tok_sb[:, 4:8], ratio_ps)
-        clip_ps = psum.tile([P, 4 * P], F32, name="clip_ps")
-        spread(clip[:, 4:8], clip_ps)
+        base_sb = keep.tile([P, U], F32, name="base_sb", align_bytes=64)
+        rho_ps = []
+        for g in range(2):
+            base_ps = psum.tile([P, 4 * P], F32, name=f"base_ps{g}", tag=f"bank{g}")
+            spread(base[:, 4 * g : 4 * g + 4], base_ps)
+            for c in range(2):
+                nc.scalar.copy(base_sb[:, 512 * g + 256 * c : 512 * g + 256 * (c + 1)], base_ps[:, 256 * c : 256 * (c + 1)])
+        for g in range(2):
+            bank = psum.tile([P, 4 * P], F32, name=f"rho_ps{g}", tag=f"bank{2 + g}")
+            spread(rho[:, 4 * g : 4 * g + 4], bank)
+            rho_ps.append(bank)
 
         def fetch(b, c0, c1):
             g = keep.tile([P, c1 - c0], F32, name=f"g{b}_{c0}", align_bytes=64)
@@ -169,7 +184,7 @@ def tile_picked_ygrpo_clip_p_kernel(tc, x_words, x_scales, w1, lr, lo, hi, offs,
         def turn(b, c0, c1):
             g = fetch(b, c0, c1)
             width = c1 - c0
-            gt = psum.tile([P, width], F32, name=f"gt{b}_{c0}", tag="work", bufs=6)
+            gt = psum.tile([P, width], F32, name=f"gt{b}_{c0}", tag=f"bank{4 + c0 // 256 % 2}")
             for i in range(width // P):
                 nc.tensor.transpose(gt[:, i * P : (i + 1) * P], g[:, i * P : (i + 1) * P], ident[:])
             over = keep.tile([P, width], F32, name=f"over{b}_{c0}", align_bytes=64)
@@ -183,7 +198,7 @@ def tile_picked_ygrpo_clip_p_kernel(tc, x_words, x_scales, w1, lr, lo, hi, offs,
 
         def turn_back(b, c0, c1, over, lin):
             width = c1 - c0
-            back = psum.tile([P, width], F32, name=f"back{b}_{c0}", tag="work", bufs=6)
+            back = psum.tile([P, width], F32, name=f"back{b}_{c0}", tag=f"bank{6 + c0 // 256 % 2}")
             for i in range(width // P):
                 cols = slice(i * P, (i + 1) * P)
                 nc.tensor.matmul(back[:, cols], over[:, cols], ident[:], start=True, stop=False, is_transpose=True)
@@ -196,28 +211,30 @@ def tile_picked_ygrpo_clip_p_kernel(tc, x_words, x_scales, w1, lr, lo, hi, offs,
             nc.sync.dma_start(out=out[P * b : P * (b + 1), c0:c1], in_=o[:])
 
         def direct(b, chunks):
-            gs_, us, vs = [fetch(b, c0, c1) for c0, c1 in chunks], [], []
-            for (c0, c1), g in zip(chunks, gs_):
+            us, vs = [], []
+            for c0, c1 in chunks:
                 u = keep.tile([P, c1 - c0], F32, name=f"u{b}_{c0}", align_bytes=64)
-                nc.vector.tensor_tensor(u[:], g[:], ratio_ps[:, c0 - 512 : c1 - 512], ALU.mult)
-                v = keep.tile([P, c1 - c0], F32, name=f"v{b}_{c0}", align_bytes=64)
-                nc.vector.tensor_tensor(v[:], g[:], clip_ps[:, c0 - 512 : c1 - 512], ALU.mult)
+                nc.vector.tensor_tensor(u[:], adv[b][:].indirect(ans_t[:, c0 // 16 : c1 // 16]), base_sb[:, c0:c1], ALU.mult)
                 us.append(u)
+            for (c0, c1), u in zip(chunks, us):
+                v = keep.tile([P, c1 - c0], F32, name=f"v{b}_{c0}", align_bytes=64)
+                g = c0 // 512
+                nc.vector.tensor_tensor(v[:], u[:], rho_ps[g][:, c0 - 512 * g : c1 - 512 * g], ALU.mult)
                 vs.append(v)
             for (c0, c1), u, v in zip(chunks, us, vs):
                 o = keep.tile([P, c1 - c0], F32, name=f"o{b}_{c0}", align_bytes=64)
                 nc.vector.tensor_tensor(o[:], u[:], v[:], ALU.min)
                 nc.sync.dma_start(out=out[P * b : P * (b + 1), c0:c1], in_=o[:])
 
-        chunks = [(0, 0, 128), (0, 128, 384), (0, 384, 640), (0, 640, 896), (0, 896, 1024), (1, 0, 256), (1, 256, 384), (1, 384, 512)]
+        chunks = [(0, c0, c0 + 256) for c0 in range(0, U, 256)]
         turned, backs = [], []
         for k in range(len(chunks) + 2):
             if k < len(chunks):
-                if chunks[k][:2] == (1, 0):
-                    normalise(1)
                 turned.append(turn(*chunks[k]))
             if 1 <= k <= len(chunks):
                 backs.append(turn_back(*turned[k - 1]))
             if k >= 2:
                 leave(*backs[k - 2])
+        normalise(1)
+        direct(1, [(0, 512)])
         direct(1, [(512, 768), (768, 1024)])

from contextlib import ExitStack

import concourse.mybir as mybir
from concourse.masks import make_identity

F32 = mybir.dt.float32
BF16 = mybir.dt.bfloat16
I32 = mybir.dt.int32
U32 = mybir.dt.uint32
U16 = mybir.dt.uint16
U8 = mybir.dt.uint8
FP8X4 = mybir.dt.float8_e4m3fn_x4
ALU = mybir.AluOpType
ACT = mybir.ActivationFunctionType
AX = mybir.AxisListType

P = 128
K, T, S, D, N, U = 1024, 1024, 512, 4, 256, 1024
PASSES = 2
HALF = S // 2
FLOPS = 2 * K * N * S
BYTES = 2 * P * T * 4 + 2 * 16 * T + K * N * 4 + 3 * U * 4 + P * (S + U) // 8 + N * U * 4


def tile_picked_ygrpo_clip_p_kernel(tc, x_words, x_scales, w1, lr, lo, hi, offs, ans, out):
    nc = tc.nc
    with ExitStack() as ctx:
        keep = ctx.enter_context(tc.tile_pool(name="keep", bufs=1))
        psum = ctx.enter_context(tc.psum_pool(name="psum", bufs=1))

        offs_t = keep.tile([P, S // 16], U16, name="offs_t")
        ans_t = keep.tile([P, U // 16], U16, name="ans_t")
        xs = keep.tile([P, T], U8, name="xs", align_bytes=64)
        xw = [keep.tile([P, T], U32, name=f"xw{o}", align_bytes=64) for o in range(PASSES)]
        wraw = [keep.tile([P, 4, N], F32, name=f"wraw{o}", align_bytes=64) for o in range(PASSES)]
        lr_rows = keep.tile([8, P], F32, name="lr_rows", align_bytes=64)
        ratio_rows = keep.tile([8, P], F32, name="ratio_rows", align_bytes=64)
        ident = keep.tile([P, P], F32, name="ident", align_bytes=64)
        adv = [keep.tile([P, S + 16 * b], F32, name=f"adv{b}", align_bytes=64) for b in range(2)]

        nc.gpsimd.memset(xs[:].bitcast(I32), 0)
        make_identity(nc, ident[:])
        nc.gpsimd.memset(adv[1][:, S:], 0.0)

        def load_x(queue, o):
            queue.dma_start(out=xw[o][:].bitcast(I32), in_=x_words[o].rearrange("p c r -> p (c r)").bitcast(I32))

        def load_w(queue, o):
            queue.dma_start(out=wraw[o][:], in_=w1[512 * o : 512 * (o + 1), :].rearrange("(p j) c -> p j c", j=4))

        nc.sync.dma_start(offs_t[:], offs)
        nc.sync.dma_start(out=lr_rows[:], in_=lr[0].rearrange("(b n) -> b n", n=P))
        load_x(nc.sync, 0)
        for q in range(4):
            nc.sync.dma_start(out=xs[32 * q : 32 * q + 8, :].bitcast(I32), in_=x_scales[:, 4 * q : 4 * q + 4, :].bitcast(I32))
        load_w(nc.sync, 0)
        load_w(nc.sync, 1)
        load_x(nc.sync, 1)
        nc.sync.dma_start(ans_t[:], ans)
        nc.scalar.activation(ratio_rows[:], lr_rows[:], ACT.Exp)
        warm = keep.tile([8, 1], F32, name="warm")
        nc.scalar.activation(warm[:], ratio_rows[:, 0:1], ACT.Abs_reciprocal_sqrt)

        wbf = [keep.tile([P, 4 * N], BF16, name=f"wbf{o}", align_bytes=64) for o in range(PASSES)]
        wq = [keep.tile([P, N], U32, name=f"wq{o}", align_bytes=64) for o in range(PASSES)]
        ws = [keep.tile([P, N], U8, name=f"ws{o}", align_bytes=64) for o in range(PASSES)]

        def weave(copy, o, c0, c1):
            copy(
                wbf[o][:, 4 * c0 : 4 * c1].rearrange("p (c i t) -> p c t i", i=4, t=4),
                wraw[o][:, :, c0:c1].rearrange("p t (c i) -> p c t i", i=4),
            )

        def quant(o, c0, c1):
            nc.vector.quantize_mx(out=wq[o][:, c0:c1].bitcast(FP8X4), scales=ws[o][:, c0:c1], in_=wbf[o][:, 4 * c0 : 4 * c1])

        gs = keep.tile([P, S], U8, name="gs", align_bytes=64)
        gw0 = keep.tile([P, S], U32, name="gw0", align_bytes=64)
        gw1 = [keep.tile([P, HALF], U32, name=f"gw1{h}", align_bytes=64) for h in range(2)]

        nc.vector.tensor_copy(gs[:], xs[:].indirect(offs_t[:]))
        nc.vector.tensor_copy(gw0[:], xw[0][:].indirect(offs_t[:]))
        weave(nc.scalar.copy, 0, 0, N)
        quant(0, 0, N)
        weave(nc.scalar.copy, 1, 0, P)
        weave(nc.vector.tensor_copy, 1, P, N)
        quant(1, 0, P)
        quant(1, P, N)
        for h in range(2):
            nc.vector.tensor_copy(gw1[h][:], xw[1][:].indirect(offs_t[:, h * HALF // 16 : (h + 1) * HALF // 16]))

        def product(acc, b, h):
            half = slice(h * HALF, (h + 1) * HALF)
            for o, words in enumerate((gw0[:, half], gw1[h][:])):
                nc.tensor.matmul_mx(
                    out=acc,
                    lhsT=wq[o][:, b * P : (b + 1) * P].bitcast(FP8X4),
                    lhsT_scale=ws[o][:, b * P : (b + 1) * P],
                    rhs=words.bitcast(FP8X4),
                    rhs_scale=gs[4 * o : P, half],
                    start=(o == 0),
                    stop=(o == PASSES - 1),
                )

        G = S // D
        y = [[psum.tile([P, HALF], F32, name=f"y{b}{h}", tag=f"bank{2 * b + h}") for h in range(2)] for b in range(2)]
        for h in range(2):
            for b in range(2):
                product(y[b][h][:], b, h)

        tok = wraw[0][:, 0, 0:P]
        nc.scalar.copy(tok[0:8, :], ratio_rows[:])
        for i, src in ((1, lo), (2, hi)):
            nc.sync.dma_start(out=tok[8 * i : 8 * i + 8, :], in_=src[0].rearrange("(b n) -> b n", n=P))
        tok_ps = psum.tile([P, P], F32, name="tok_ps", tag="bank4")
        nc.tensor.transpose(tok_ps[:], tok, ident[:])
        tok_sb = keep.tile([P, 24], F32, name="tok_sb")
        nc.scalar.copy(tok_sb[:], tok_ps[:, 0:24])

        sums = [[keep.tile([P, G // 2], F32, name=f"sums{b}{h}") for h in range(2)] for b in range(2)]
        dd = [keep.tile([P, G, D], F32, name=f"dd{b}") for b in range(2)]
        d2 = [keep.tile([P, G, D], F32, name=f"d2{b}") for b in range(2)]
        var = [keep.tile([P, G], F32, name=f"var{b}") for b in range(2)]
        rs = [keep.tile([P, G], F32, name=f"rs{b}") for b in range(2)]
        for h in range(2):
            for b in range(2):
                nc.vector.tensor_reduce(sums[b][h][:], y[b][h][:].rearrange("p (v d) -> p v d", d=D), AX.X, ALU.add)
        ratio = tok_sb[:, 0:8]
        above = keep.tile([P, 8], F32, name="above")
        clip = keep.tile([P, 8], F32, name="clip")
        kappa = keep.tile([P, 8], F32, name="kappa")
        neg_clip = keep.tile([P, 8], F32, name="neg_clip")
        tiny = keep.tile([P, 8], F32, name="tiny")
        base = keep.tile([P, 8], F32, name="base")
        inv = keep.tile([P, 8], F32, name="inv")
        rho = keep.tile([P, 8], F32, name="rho")
        nc.vector.tensor_tensor(above[:], ratio, tok_sb[:, 8:16], ALU.max)
        nc.vector.tensor_tensor(clip[:], above[:], tok_sb[:, 16:24], ALU.min)
        nc.vector.tensor_scalar(tiny[:], clip[:], 0.0, 2.0**-64, ALU.is_equal, ALU.mult)
        nc.vector.tensor_tensor(kappa[:], clip[:], ratio, ALU.subtract)
        nc.vector.tensor_tensor(base[:], clip[:], tiny[:], ALU.add)
        nc.scalar.mul(neg_clip[:], clip[:], -1.0)
        nc.vector.reciprocal(inv[:], base[:])
        nc.vector.tensor_tensor(rho[:], ratio, inv[:], ALU.mult)
        for b in range(2):
            for h in range(2):
                groups = slice(h * G // 2, (h + 1) * G // 2)
                nc.vector.scalar_tensor_tensor(
                    dd[b][:, groups, :], sums[b][h][:].unsqueeze(2).to_broadcast([P, G // 2, D]), -1.0 / D,
                    y[b][h][:].rearrange("p (v d) -> p v d", d=D), ALU.mult, ALU.add,
                )
                nc.scalar.activation(d2[b][:, groups, :], dd[b][:, groups, :], ACT.Square, scale=0.5)
        for b in range(2):
            nc.vector.tensor_reduce(var[b][:], d2[b][:], AX.X, ALU.add)
            nc.scalar.activation(rs[b][:], var[b][:], ACT.Abs_reciprocal_sqrt, bias=0.1)

        def normalise(b):
            nc.vector.tensor_tensor(
                adv[b][:, 0:S].rearrange("p (v d) -> p v d", d=D), dd[b][:], rs[b][:].unsqueeze(2).to_broadcast([P, G, D]), ALU.mult
            )

        normalise(0)
        def spread(col, bank):
            for i in range(4):
                nc.tensor.transpose(bank[:, i * P : (i + 1) * P], col[:, i : i + 1].to_broadcast([P, P]), ident[:])

        base_sb = keep.tile([P, U], F32, name="base_sb", align_bytes=64)
        rho_ps = []
        for g in range(2):
            base_ps = psum.tile([P, 4 * P], F32, name=f"base_ps{g}", tag=f"bank{g}")
            spread(base[:, 4 * g : 4 * g + 4], base_ps)
            for c in range(2):
                nc.scalar.copy(base_sb[:, 512 * g + 256 * c : 512 * g + 256 * (c + 1)], base_ps[:, 256 * c : 256 * (c + 1)])
        for g in range(2):
            bank = psum.tile([P, 4 * P], F32, name=f"rho_ps{g}", tag=f"bank{2 + g}")
            spread(rho[:, 4 * g : 4 * g + 4], bank)
            rho_ps.append(bank)

        def fetch(b, c0, c1):
            g = keep.tile([P, c1 - c0], F32, name=f"g{b}_{c0}", align_bytes=64)
            nc.vector.tensor_copy(g[:], adv[b][:].indirect(ans_t[:, c0 // 16 : c1 // 16]))
            return g

        def turn(b, c0, c1):
            g = fetch(b, c0, c1)
            width = c1 - c0
            gt = psum.tile([P, width], F32, name=f"gt{b}_{c0}", tag=f"bank{4 + c0 // 256 % 2}")
            for i in range(width // P):
                nc.tensor.transpose(gt[:, i * P : (i + 1) * P], g[:, i * P : (i + 1) * P], ident[:])
            over = keep.tile([P, width], F32, name=f"over{b}_{c0}", align_bytes=64)
            lin = keep.tile([P, width], F32, name=f"lin{b}_{c0}", align_bytes=64)
            for i in range(width // P):
                t = c0 // P + i
                cols = slice(i * P, (i + 1) * P)
                nc.scalar.activation(over[:, cols], gt[:, cols], ACT.Relu, scale=kappa[:, t : t + 1])
                nc.scalar.activation(lin[:, cols], gt[:, cols], ACT.Copy, scale=neg_clip[:, t : t + 1])
            return b, c0, c1, over, lin

        def turn_back(b, c0, c1, over, lin):
            width = c1 - c0
            back = psum.tile([P, width], F32, name=f"back{b}_{c0}", tag=f"bank{6 + c0 // 256 % 2}")
            for i in range(width // P):
                cols = slice(i * P, (i + 1) * P)
                nc.tensor.matmul(back[:, cols], over[:, cols], ident[:], start=True, stop=False, is_transpose=True)
                nc.tensor.matmul(back[:, cols], lin[:, cols], ident[:], start=False, stop=True, is_transpose=True)
            return b, c0, c1, back

        def leave(b, c0, c1, back):
            o = keep.tile([P, c1 - c0], F32, name=f"o{b}_{c0}", align_bytes=64)
            nc.scalar.mul(o[:], back[:], -1.0)
            nc.sync.dma_start(out=out[P * b : P * (b + 1), c0:c1], in_=o[:])

        def direct(b, chunks):
            us, vs = [], []
            for c0, c1 in chunks:
                u = keep.tile([P, c1 - c0], F32, name=f"u{b}_{c0}", align_bytes=64)
                nc.vector.tensor_tensor(u[:], adv[b][:].indirect(ans_t[:, c0 // 16 : c1 // 16]), base_sb[:, c0:c1], ALU.mult)
                us.append(u)
            for (c0, c1), u in zip(chunks, us):
                v = keep.tile([P, c1 - c0], F32, name=f"v{b}_{c0}", align_bytes=64)
                g = c0 // 512
                nc.vector.tensor_tensor(v[:], u[:], rho_ps[g][:, c0 - 512 * g : c1 - 512 * g], ALU.mult)
                vs.append(v)
            for (c0, c1), u, v in zip(chunks, us, vs):
                o = keep.tile([P, c1 - c0], F32, name=f"o{b}_{c0}", align_bytes=64)
                nc.vector.tensor_tensor(o[:], u[:], v[:], ALU.min)
                nc.sync.dma_start(out=out[P * b : P * (b + 1), c0:c1], in_=o[:])

        chunks = [(0, c0, c0 + 256) for c0 in range(0, U, 256)]
        turned, backs = [], []
        for k in range(len(chunks) + 2):
            if k < len(chunks):
                turned.append(turn(*chunks[k]))
            if 1 <= k <= len(chunks):
                backs.append(turn_back(*turned[k - 1]))
            if k >= 2:
                leave(*backs[k - 2])
        normalise(1)
        direct(1, [(0, 512)])
        direct(1, [(512, 768), (768, 1024)])
